import numpy as np
import ml_dtypes


def mxq(x, axis, fmt="e4m3"):
    dtype, down = {"e4m3": (ml_dtypes.float8_e4m3fn, 7), "e5m2": (ml_dtypes.float8_e5m2, 14)}[fmt]
    v = np.moveaxis(np.asarray(x, np.float32).astype(ml_dtypes.bfloat16).astype(np.float64), axis, -1)
    blocks = v.reshape(v.shape[:-1] + (-1, 32))
    amax = np.abs(blocks).max(-1, keepdims=True)
    byte = np.maximum(np.where(amax > 0, np.frexp(amax)[1] - 1 + 127, 0) - down, 1)
    scale = np.exp2(byte - 127.0)
    codes = (blocks / scale).astype(np.float32).astype(dtype).astype(np.float64)
    return np.moveaxis((codes * scale).reshape(v.shape), -1, axis)


WIDE = False


def mx_kscale(k):
    if not WIDE:
        return np.ones(k)
    levels = np.array([10, -10, 5, -5, 0])
    if k % 512:
        return np.exp2(np.random.permutation(np.resize(levels, k // 32))).repeat(32)
    a = np.empty((k // 512, 16))
    for p in range(k // 512):
        a[p, :8] = np.random.permutation(np.resize(levels, 8))
        for g in range(8):
            far = levels[np.abs(levels - a[p, g]) >= 10]
            a[p, g + 8] = far[np.random.randint(len(far))]
    return np.exp2(a.ravel()).repeat(32)


BF16 = ml_dtypes.bfloat16


def bf(x):
    return np.asarray(x, np.float32).astype(BF16)


def f64(x):
    return np.asarray(x).astype(np.float64)

def planes(Y):
    n, m = Y.shape
    b = f64(bf(Y)).reshape(n // 32, 32, m)
    amax = np.abs(b).max(1)
    byte = np.clip(np.where(amax > 0, np.frexp(amax)[1] - 1 + 127 - 7, 1), 1, 254)
    codes = (b * np.exp2(127.0 - byte)[:, None, :]).reshape(n, m).astype(np.float32).astype(ml_dtypes.float8_e4m3fn).view(np.uint8)
    words = codes.reshape(n // 512, 128, 4, m).transpose(0, 1, 3, 2)
    return np.ascontiguousarray(words), np.ascontiguousarray(byte.astype(np.uint8).reshape(n // 512, 16, m))


D, P, S = 3072, 1536, 512


def setup_inputs():
    s = mx_kscale(P)
    jacobian = np.random.randn(D, P) / np.sqrt(P) * s[None, :]
    step = np.random.randn(P, S) / s[:, None]
    residual = 0.8 * np.random.randn(D, S)
    weight = np.exp(0.8 * np.random.randn(D))
    return {"jacobian": bf(jacobian), "step": bf(step),
            "residual": bf(residual), "weight": bf(weight)}

def reference(jacobian, step, residual, weight):
    J = mxq(f64(jacobian), 1, "e4m3")
    V = mxq(f64(step), 0, "e4m3")
    change = J @ V
    y = f64(weight)[:, None] * (change + f64(residual))
    Y = y.reshape(D, S)
    words, scales = planes(Y)
    return y, words, scales

@@ -1,0 +1,251 @@
+from contextlib import ExitStack
+
+import concourse.mybir as mybir
+from concourse.masks import make_identity
+
+D, K, S = 3072, 1536, 512
+FLOPS = 2 * D * K * S
+
+F32 = mybir.dt.float32
+BF16 = mybir.dt.bfloat16
+I32 = mybir.dt.int32
+U32 = mybir.dt.uint32
+U8 = mybir.dt.uint8
+FP8X4 = mybir.dt.float8_e4m3fn_x4
+COPY = mybir.ActivationFunctionType.Copy
+MULT = mybir.AluOpType.mult
+ADD = mybir.AluOpType.add
+
+P = 128
+PACK = 4
+K_PASS = P * PACK
+PASSES = K // K_PASS
+GROUPS = D // K_PASS
+PAIRS = 2 * GROUPS
+HALF = S // 2
+
+
+def tile_weighted_linearised_residual_g2_kernel(tc, jacobian, step, residual, weight, out_0, out_1, out_2):
+    nc = tc.nc
+    with ExitStack() as ctx:
+        keep = ctx.enter_context(tc.tile_pool(name="keep", bufs=1))
+        j_stage = ctx.enter_context(tc.tile_pool(name="j_stage", bufs=4))
+        j_quant = ctx.enter_context(tc.tile_pool(name="j_quant", bufs=8))
+        y_stage = ctx.enter_context(tc.tile_pool(name="y_stage", bufs=3))
+        turn_psum = ctx.enter_context(tc.psum_pool(name="turn_psum", bufs=4))
+        acc_psum = ctx.enter_context(tc.psum_pool(name="acc_psum", bufs=4))
+        ctx.enter_context(tc.manual_schedule())
+
+        ident = keep.tile([P, P], F32, name="ident")
+        w_rows = keep.tile([P, K_PASS], BF16, name="w_rows")
+        w_cols = keep.tile([P, GROUPS, PACK], F32, name="w_cols")
+        j_raw = [keep.tile([P, 2, K], BF16, name="j_raw%d" % i) for i in range(PAIRS)]
+        v_raw = [keep.tile([P, PACK, S], BF16, name="v_raw%d" % c) for c in range(PASSES)]
+        v_grouped = [keep.tile([P, S, PACK], BF16, name="v_grouped%d" % c, align_bytes=64) for c in range(PASSES)]
+        v_codes = [keep.tile([P, S], U32, name="v_codes%d" % c, align_bytes=64) for c in range(PASSES)]
+        v_scales = [keep.tile([P, S], U8, name="v_scales%d" % c, align_bytes=64) for c in range(PASSES)]
+        r_raw = [keep.tile([P, PACK, S], BF16, name="r_raw%d" % g) for g in range(GROUPS)]
+        y = [keep.tile([P, PACK, S], F32, name="y%d" % g) for g in range(GROUPS)]
+        y_codes = [keep.tile([P, S], U32, name="y_codes%d" % g, align_bytes=64) for g in range(GROUPS)]
+        y_scales = keep.tile([P, GROUPS, S], U8, name="y_scales", align_bytes=64)
+
+        def group_rows(dram, g):
+            return dram[g * K_PASS:(g + 1) * K_PASS, :].rearrange("(p t) c -> p t c", t=PACK)
+
+        def load_j(pair, lo, hi):
+            g, t0 = divmod(2 * pair, PACK)
+            nc.sync.dma_start(out=j_raw[pair][:, lo:hi, :], in_=group_rows(jacobian, g)[:, t0 + lo:t0 + hi, :])
+
+        def load_v(c):
+            nc.sync.dma_start(out=v_raw[c][:], in_=group_rows(step, c))
+
+        def load_r(g):
+            nc.sync.dma_start(out=r_raw[g][:], in_=group_rows(residual, g))
+
+        turned = {}
+        grouped = {}
+        j_codes = {}
+        j_scales = {}
+        acc = {}
+        y_grouped = {}
+
+        def turn(unit):
+            bank = turn_psum.tile([P, 2, 2, P], F32, name="bank")
+            turned[unit] = bank
+            for h in range(2):
+                tile, c = divmod(2 * unit + h, PASSES)
+                words = j_raw[tile // 2][:, tile % 2, :].bitcast(F32)
+                for u in range(2):
+                    nc.tensor.transpose(bank[:, h, u, :], words[:, 256 * c + u:256 * (c + 1):2], ident[:])
+
+        def empty(unit):
+            dst = j_stage.tile([P, 2 * K_PASS], BF16, name="j_grouped", align_bytes=64)
+            grouped[unit] = dst
+            nc.scalar.copy(
+                out=dst[:].bitcast(F32).rearrange("p (h d u) -> p h d u", h=2, u=2),
+                in_=turned[unit][:].rearrange("p h u d -> p h d u"),
+            )
+
+        def quantise_j(unit):
+            codes = j_quant.tile([P, 2 * P], U32, name="j_codes", align_bytes=64)
+            scales = j_quant.tile([P, 2 * P], U8, name="j_scales", align_bytes=64)
+            j_codes[unit] = codes
+            j_scales[unit] = scales
+            nc.vector.quantize_mx(out=codes[:].bitcast(FP8X4), scales=scales[:], in_=grouped[unit][:])
+
+        def interleave_v(c):
+            nc.vector.tensor_copy(
+                out=v_grouped[c][:].rearrange("p (n i) t -> p n t i", i=4),
+                in_=v_raw[c][:].rearrange("p t (n i) -> p n t i", i=4),
+            )
+
+        def quantise_v(c):
+            nc.vector.quantize_mx(
+                out=v_codes[c][:].bitcast(FP8X4),
+                scales=v_scales[c][:],
+                in_=v_grouped[c][:].rearrange("p n t -> p (n t)"),
+            )
+
+        def multiply(tile, c):
+            if c == 0:
+                acc[tile] = acc_psum.tile([P, S], F32, name="acc")
+            unit, h = divmod(PASSES * tile + c, 2)
+            cols = slice(h * P, (h + 1) * P)
+            nc.tensor.matmul_mx(
+                out=acc[tile][:],
+                lhsT=j_codes[unit][:, cols].bitcast(FP8X4),
+                lhsT_scale=j_scales[unit][:, cols],
+                rhs=v_codes[c][:].bitcast(FP8X4),
+                rhs_scale=v_scales[c][:],
+                start=(c == 0),
+                stop=(c == PASSES - 1),
+            )
+
+        def weigh_residual(tile):
+            g, t = divmod(tile, PACK)
+            nc.scalar.activation(out=y[g][:, t, :], in_=r_raw[g][:, t, :], func=COPY, scale=w_cols[:, g, t:t + 1])
+
+        def finish(tile):
+            g, t = divmod(tile, PACK)
+            nc.vector.scalar_tensor_tensor(
+                out=y[g][:, t, :], in0=acc[tile][:], scalar=w_cols[:, g, t:t + 1], in1=y[g][:, t, :], op0=MULT, op1=ADD
+            )
+
+        def interleave_y(half, copy):
+            g, h = divmod(half, 2)
+            dst = y_stage.tile([P, HALF, PACK], BF16, name="y_grouped", align_bytes=64)
+            y_grouped[half] = dst
+            copy(
+                out=dst[:].rearrange("p (n i) t -> p n t i", i=4),
+                in_=y[g][:, :, h * HALF:(h + 1) * HALF].rearrange("p t (n i) -> p n t i", i=4),
+            )
+
+        def quantise_y(half):
+            g, h = divmod(half, 2)
+            cols = slice(h * HALF, (h + 1) * HALF)
+            nc.vector.quantize_mx(
+                out=y_codes[g][:, cols].bitcast(FP8X4),
+                scales=y_scales[:, g, cols],
+                in_=y_grouped[half][:].rearrange("p n t -> p (n t)"),
+            )
+
+        def store_y(g, lo, hi):
+            nc.sync.dma_start(out=group_rows(out_0, g)[:, lo:hi, :], in_=y[g][:, lo:hi, :])
+
+        def store_codes(g):
+            nc.sync.dma_start(
+                out=out_1[g].rearrange("p m t -> p (m t)").bitcast(I32), in_=y_codes[g][:].bitcast(I32)
+            )
+
+        nc.gpsimd.memset(w_rows[:], 0.0)
+        make_identity(nc, ident[:])
+        nc.scalar.dma_start(out=w_rows[0:GROUPS, :], in_=weight.rearrange("(g d) -> g d", g=GROUPS))
+        load_v(0)
+        load_j(0, 0, 1)
+        load_v(1)
+        load_j(0, 1, 2)
+        load_v(2)
+        load_j(1, 0, 2)
+        for g in range(GROUPS):
+            load_r(g)
+            for pair in (2 * g + 2, 2 * g + 3):
+                if pair < PAIRS:
+                    load_j(pair, 0, 2)
+
+        interleave_v(0)
+        quantise_v(0)
+        interleave_v(1)
+        for unit in range(3):
+            turn(unit)
+            empty(unit)
+        w_bank = turn_psum.tile([P, 2, 2, P], F32, name="bank")
+        w_words = w_rows[:].bitcast(F32)
+        for u in range(2):
+            nc.tensor.transpose(w_bank[:, 0, u, :], w_words[:, u:256:2], ident[:])
+        nc.scalar.activation(
+            out=w_cols[:].rearrange("p g (u e) -> p u g e", u=2),
+            in_=w_bank[:].rearrange("p h u r -> p (h u r)").bitcast(BF16)
+            .rearrange("p (h u r e) -> p h u r e", h=2, u=2, e=2)[:, 0, :, 0:GROUPS, :],
+            func=COPY,
+        )
+        quantise_j(0)
+        quantise_v(1)
+        quantise_j(1)
+        quantise_j(2)
+        multiply(0, 0)
+        multiply(0, 1)
+        multiply(1, 0)
+        multiply(1, 1)
+        interleave_v(2)
+        quantise_v(2)
+
+        for i in range(PAIRS):
+            a, b = 2 * i, 2 * i + 1
+            units = [3 * (i + 1) + n for n in range(3)] if i + 1 < PAIRS else []
+            if i > 0:
+                weigh_residual(a)
+            for unit in units:
+                turn(unit)
+                empty(unit)
+            if i == 0:
+                weigh_residual(a)
+            weigh_residual(b)
+            if i > 0:
+                finish(a - 1)
+                store_y((i - 1) // 2, 2 * ((i - 1) % 2), 2 * ((i - 1) % 2) + 2)
+            if i >= 3:
+                quantise_y(i - 3)
+                if i % 2 == 0:
+                    store_codes((i - 3) // 2)
+            if units:
+                quantise_j(units[0])
+            if i >= 2:
+                interleave_y(i - 2, nc.vector.tensor_copy)
+            for unit in units[1:]:
+                quantise_j(unit)
+            if i == 0:
+                multiply(a, 2)
+                multiply(b, 2)
+            else:
+                for tile in (a, b):
+                    for c in range(PASSES):
+                        multiply(tile, c)
+            finish(a)
+
+        last = GROUPS - 1
+        store_y(last, 2, 3)
+        quantise_y(PAIRS - 3)
+        store_codes(last - 1)
+        finish(2 * PAIRS - 1)
+        store_y(last, 3, 4)
+        interleave_y(PAIRS - 1, nc.scalar.copy)
+        interleave_y(PAIRS - 2, nc.vector.tensor_copy)
+        quantise_y(PAIRS - 2)
+        quantise_y(PAIRS - 1)
+        store_codes(last)
+        scale_rows = out_2.bitcast(I32)
+        for q in range(4):
+            nc.scalar.dma_start(
+                out=scale_rows[:, 4 * q:4 * q + 4, :].rearrange("g r m -> r g m"),
+                in_=y_scales[32 * q:32 * q + 4, :, :].bitcast(I32),
+            )

@@ -59,8 +59,8 @@ def tile_weighted_linearised_residual_g2_kernel(tc, jacobian, step, residual, we
         def load_v(c):
             nc.sync.dma_start(out=v_raw[c][:], in_=group_rows(step, c))
 
-        def load_r(g):
-            nc.sync.dma_start(out=r_raw[g][:], in_=group_rows(residual, g))
+        def load_r(g, lo, hi):
+            nc.sync.dma_start(out=r_raw[g][:, lo:hi, :], in_=group_rows(residual, g)[:, lo:hi, :])
 
         turned = {}
         grouped = {}
@@ -93,10 +93,10 @@ def tile_weighted_linearised_residual_g2_kernel(tc, jacobian, step, residual, we
             j_scales[unit] = scales
             nc.vector.quantize_mx(out=codes[:].bitcast(FP8X4), scales=scales[:], in_=grouped[unit][:])
 
-        def interleave_v(c):
-            nc.vector.tensor_copy(
-                out=v_grouped[c][:].rearrange("p (n i) t -> p n t i", i=4),
-                in_=v_raw[c][:].rearrange("p t (n i) -> p n t i", i=4),
+        def interleave_v(c, lo, hi, copy):
+            copy(
+                out=v_grouped[c][:, lo:hi, :].rearrange("p (n i) t -> p n t i", i=4),
+                in_=v_raw[c][:, :, lo:hi].rearrange("p t (n i) -> p n t i", i=4),
             )
 
         def quantise_v(c):
@@ -106,17 +106,17 @@ def tile_weighted_linearised_residual_g2_kernel(tc, jacobian, step, residual, we
                 in_=v_grouped[c][:].rearrange("p n t -> p (n t)"),
             )
 
-        def multiply(tile, c):
-            if c == 0:
-                acc[tile] = acc_psum.tile([P, S], F32, name="acc")
+        def multiply(tile, c, lo=0, hi=S):
+            if (tile, lo) not in acc:
+                acc[tile, lo] = acc_psum.tile([P, hi - lo], F32, name="acc")
             unit, h = divmod(PASSES * tile + c, 2)
             cols = slice(h * P, (h + 1) * P)
             nc.tensor.matmul_mx(
-                out=acc[tile][:],
+                out=acc[tile, lo][:],
                 lhsT=j_codes[unit][:, cols].bitcast(FP8X4),
                 lhsT_scale=j_scales[unit][:, cols],
-                rhs=v_codes[c][:].bitcast(FP8X4),
-                rhs_scale=v_scales[c][:],
+                rhs=v_codes[c][:, lo:hi].bitcast(FP8X4),
+                rhs_scale=v_scales[c][:, lo:hi],
                 start=(c == 0),
                 stop=(c == PASSES - 1),
             )
@@ -125,10 +125,11 @@ def tile_weighted_linearised_residual_g2_kernel(tc, jacobian, step, residual, we
             g, t = divmod(tile, PACK)
             nc.scalar.activation(out=y[g][:, t, :], in_=r_raw[g][:, t, :], func=COPY, scale=w_cols[:, g, t:t + 1])
 
-        def finish(tile):
+        def finish(tile, lo=0, hi=S):
             g, t = divmod(tile, PACK)
             nc.vector.scalar_tensor_tensor(
-                out=y[g][:, t, :], in0=acc[tile][:], scalar=w_cols[:, g, t:t + 1], in1=y[g][:, t, :], op0=MULT, op1=ADD
+                out=y[g][:, t, lo:hi], in0=acc[tile, lo][:], scalar=w_cols[:, g, t:t + 1], in1=y[g][:, t, lo:hi],
+                op0=MULT, op1=ADD,
             )
 
         def interleave_y(half, copy):
@@ -149,103 +150,150 @@ def tile_weighted_linearised_residual_g2_kernel(tc, jacobian, step, residual, we
                 in_=y_grouped[half][:].rearrange("p n t -> p (n t)"),
             )
 
-        def store_y(g, lo, hi):
-            nc.sync.dma_start(out=group_rows(out_0, g)[:, lo:hi, :], in_=y[g][:, lo:hi, :])
+        def store_y(g, lo, hi, c0=0, c1=S):
+            nc.sync.dma_start(out=group_rows(out_0, g)[:, lo:hi, c0:c1], in_=y[g][:, lo:hi, c0:c1])
 
-        def store_codes(g):
+        def store_codes(g, lo=0, hi=S):
             nc.sync.dma_start(
-                out=out_1[g].rearrange("p m t -> p (m t)").bitcast(I32), in_=y_codes[g][:].bitcast(I32)
+                out=out_1[g].rearrange("p m t -> p (m t)").bitcast(I32)[:, lo:hi], in_=y_codes[g][:, lo:hi].bitcast(I32)
+            )
+
+        def store_scales(queue, g_lo, g_hi, quadrants=(0, 1, 2, 3)):
+            scale_rows = out_2.bitcast(I32)
+            for q in quadrants:
+                queue.dma_start(
+                    out=scale_rows[g_lo:g_hi, 4 * q:4 * q + 4, :].rearrange("g r m -> r g m"),
+                    in_=y_scales[32 * q:32 * q + 4, g_lo:g_hi, :].bitcast(I32),
+                )
+
+        def turn_weights():
+            w_bank = turn_psum.tile([P, 2, 2, P], F32, name="bank")
+            w_words = w_rows[:].bitcast(F32)
+            for u in range(2):
+                nc.tensor.transpose(w_bank[:, 0, u, :], w_words[:, u:256:2], ident[:])
+            nc.scalar.activation(
+                out=w_cols[:].rearrange("p g (u e) -> p u g e", u=2),
+                in_=w_bank[:].rearrange("p h u r -> p (h u r)").bitcast(BF16)
+                .rearrange("p (h u r e) -> p h u r e", h=2, u=2, e=2)[:, 0, :, 0:GROUPS, :],
+                func=COPY,
             )
 
         nc.gpsimd.memset(w_rows[:], 0.0)
         make_identity(nc, ident[:])
         nc.scalar.dma_start(out=w_rows[0:GROUPS, :], in_=weight.rearrange("(g d) -> g d", g=GROUPS))
-        load_v(0)
         load_j(0, 0, 1)
-        load_v(1)
+        load_v(0)
         load_j(0, 1, 2)
+        load_j(1, 0, 1)
+        load_v(1)
+        load_j(1, 1, 2)
         load_v(2)
-        load_j(1, 0, 2)
-        for g in range(GROUPS):
-            load_r(g)
+        load_j(2, 0, 2)
+        load_r(0, 0, 4)
+        load_j(3, 0, 2)
+        for g in range(1, GROUPS):
             for pair in (2 * g + 2, 2 * g + 3):
                 if pair < PAIRS:
                     load_j(pair, 0, 2)
+                if pair % 2 == 0:
+                    load_r(g, 0, 4)
 
-        interleave_v(0)
+        SPLIT = 192
+        turn_weights()
+        turn(0)
+        empty(0)
+        quantise_j(0)
+        interleave_v(0, 0, SPLIT, nc.scalar.copy)
+        interleave_v(0, SPLIT, S, nc.vector.tensor_copy)
         quantise_v(0)
-        interleave_v(1)
-        for unit in range(3):
+        for unit in (1, 2, 3):
             turn(unit)
             empty(unit)
-        w_bank = turn_psum.tile([P, 2, 2, P], F32, name="bank")
-        w_words = w_rows[:].bitcast(F32)
-        for u in range(2):
-            nc.tensor.transpose(w_bank[:, 0, u, :], w_words[:, u:256:2], ident[:])
-        nc.scalar.activation(
-            out=w_cols[:].rearrange("p g (u e) -> p u g e", u=2),
-            in_=w_bank[:].rearrange("p h u r -> p (h u r)").bitcast(BF16)
-            .rearrange("p (h u r e) -> p h u r e", h=2, u=2, e=2)[:, 0, :, 0:GROUPS, :],
-            func=COPY,
-        )
-        quantise_j(0)
-        quantise_v(1)
-        quantise_j(1)
-        quantise_j(2)
+            quantise_j(unit)
         multiply(0, 0)
-        multiply(0, 1)
         multiply(1, 0)
+        multiply(2, 0)
+        interleave_v(1, 0, SPLIT, nc.scalar.copy)
+        interleave_v(1, SPLIT, S, nc.vector.tensor_copy)
+        quantise_v(1)
+        for unit in (4, 5):
+            turn(unit)
+            empty(unit)
+            quantise_j(unit)
+        multiply(0, 1)
         multiply(1, 1)
-        interleave_v(2)
+        multiply(2, 1)
+        multiply(3, 0)
+        multiply(3, 1)
+        interleave_v(2, 0, SPLIT, nc.scalar.copy)
+        interleave_v(2, SPLIT, S, nc.vector.tensor_copy)
         quantise_v(2)
+        for unit in (6, 7, 8):
+            turn(unit)
+            empty(unit)
+            quantise_j(unit)
+        for tile in range(4):
+            multiply(tile, 2)
+        for tile in range(3):
+            weigh_residual(tile)
+            finish(tile)
+        store_y(0, 0, 2)
+        weigh_residual(3)
 
-        for i in range(PAIRS):
+        weighed = 4
+        last = GROUPS - 1
+        for i in range(2, PAIRS - 1):
             a, b = 2 * i, 2 * i + 1
-            units = [3 * (i + 1) + n for n in range(3)] if i + 1 < PAIRS else []
-            if i > 0:
-                weigh_residual(a)
+            units = [3 * (i + 1) + n for n in range(3)]
+            if 2 < i and weighed < 2 * PAIRS:
+                weigh_residual(weighed)
+                weighed += 1
             for unit in units:
                 turn(unit)
                 empty(unit)
-            if i == 0:
-                weigh_residual(a)
-            weigh_residual(b)
-            if i > 0:
-                finish(a - 1)
-                store_y((i - 1) // 2, 2 * ((i - 1) % 2), 2 * ((i - 1) % 2) + 2)
-            if i >= 3:
-                quantise_y(i - 3)
-                if i % 2 == 0:
-                    store_codes((i - 3) // 2)
-            if units:
-                quantise_j(units[0])
-            if i >= 2:
-                interleave_y(i - 2, nc.vector.tensor_copy)
+            for n in range(2 if i % 2 == 0 else 1):
+                if weighed < 2 * PAIRS:
+                    weigh_residual(weighed)
+                    weighed += 1
+            finish(a - 1)
+            store_y((i - 1) // 2, 2 * ((i - 1) % 2), 2 * ((i - 1) % 2) + 2)
+            interleave_y(i - 2, nc.vector.tensor_copy)
+            if i == PAIRS - 2:
+                interleave_y(i - 1, nc.scalar.copy)
+            quantise_j(units[0])
+            quantise_y(i - 2)
+            if i % 2 == 1:
+                store_codes((i - 2) // 2)
+            if i == PAIRS - 3:
+                store_scales(nc.sync, 0, last - 1)
             for unit in units[1:]:
                 quantise_j(unit)
-            if i == 0:
-                multiply(a, 2)
-                multiply(b, 2)
-            else:
-                for tile in (a, b):
-                    for c in range(PASSES):
-                        multiply(tile, c)
+            for tile in (a, b):
+                for c in range(PASSES):
+                    multiply(tile, c)
             finish(a)
 
-        last = GROUPS - 1
-        store_y(last, 2, 3)
+        a, b = 2 * PAIRS - 2, 2 * PAIRS - 1
+        store_y(last, 0, 1)
+        finish(a - 1)
+        store_y(last, 1, 2)
+        for lo in (0, HALF):
+            for tile in (a, b):
+                for c in range(PASSES):
+                    multiply(tile, c, lo, lo + HALF)
+        finish(a, 0, HALF)
+        finish(b, 0, HALF)
+        interleave_y(PAIRS - 2, nc.scalar.copy)
+        store_y(last, 2, 4, 0, HALF)
         quantise_y(PAIRS - 3)
         store_codes(last - 1)
-        finish(2 * PAIRS - 1)
-        store_y(last, 3, 4)
-        interleave_y(PAIRS - 1, nc.scalar.copy)
-        interleave_y(PAIRS - 2, nc.vector.tensor_copy)
+        finish(a, HALF, S)
+        finish(b, HALF, S)
+        store_y(last, 2, 4, HALF, S)
+        interleave_y(PAIRS - 1, nc.vector.tensor_copy)
         quantise_y(PAIRS - 2)
+        store_codes(last, 0, HALF)
         quantise_y(PAIRS - 1)
-        store_codes(last)
-        scale_rows = out_2.bitcast(I32)
-        for q in range(4):
-            nc.scalar.dma_start(
-                out=scale_rows[:, 4 * q:4 * q + 4, :].rearrange("g r m -> r g m"),
-                in_=y_scales[32 * q:32 * q + 4, :, :].bitcast(I32),
-            )
+        store_codes(last, HALF, S)
+        store_scales(nc.scalar, last - 1, GROUPS, (0, 1))
+        store_scales(nc.sync, last - 1, GROUPS, (2, 3))

@@ -178,11 +178,13 @@ def tile_weighted_linearised_residual_g2_kernel(tc, jacobian, step, residual, we
                 func=COPY,
             )
 
-        nc.gpsimd.memset(w_rows[:], 0.0)
+        nc.vector.memset(w_rows[:].bitcast(I32), 0)
         make_identity(nc, ident[:])
-        nc.scalar.dma_start(out=w_rows[0:GROUPS, :], in_=weight.rearrange("(g d) -> g d", g=GROUPS))
         load_j(0, 0, 1)
         load_v(0)
+        w_by_group = weight.rearrange("(g d) -> g d", g=GROUPS)
+        nc.sync.dma_start(out=w_rows[0:4, :], in_=w_by_group[0:4, :])
+        nc.sync.dma_start(out=w_rows[4:GROUPS, :], in_=w_by_group[4:GROUPS, :])
         load_j(0, 1, 2)
         load_j(1, 0, 1)
         load_v(1)
@@ -199,13 +201,13 @@ def tile_weighted_linearised_residual_g2_kernel(tc, jacobian, step, residual, we
                     load_r(g, 0, 4)
 
         SPLIT = 192
-        turn_weights()
         turn(0)
         empty(0)
         quantise_j(0)
         interleave_v(0, 0, SPLIT, nc.scalar.copy)
         interleave_v(0, SPLIT, S, nc.vector.tensor_copy)
         quantise_v(0)
+        turn_weights()
         for unit in (1, 2, 3):
             turn(unit)
             empty(unit)

@@ -18,28 +18,38 @@ ADD = mybir.AluOpType.add
 
 P = 128
 PACK = 4
-K_PASS = P * PACK
-PASSES = K // K_PASS
-GROUPS = D // K_PASS
-PAIRS = 2 * GROUPS
+SPAN = P * PACK
+PASS_WORDS = SPAN // 2
+PASSES = K // SPAN
+GROUPS = D // SPAN
+TILES = GROUPS * PACK
+UNITS = TILES * PASSES // 2
 HALF = S // 2
+LAST = GROUPS - 1
+
+RUN = 4
+HEAD_TILES = 4
+HEAD_UNITS = 9
+WEIGH_PER_RUN = 3
+HEAD_WEIGH_ON_VECTOR = 2
+V_SPLIT = 224
 
 
 def tile_weighted_linearised_residual_g2_kernel(tc, jacobian, step, residual, weight, out_0, out_1, out_2):
     nc = tc.nc
     with ExitStack() as ctx:
         keep = ctx.enter_context(tc.tile_pool(name="keep", bufs=1))
-        j_stage = ctx.enter_context(tc.tile_pool(name="j_stage", bufs=4))
-        j_quant = ctx.enter_context(tc.tile_pool(name="j_quant", bufs=8))
+        j_stage = ctx.enter_context(tc.tile_pool(name="j_stage", bufs=RUN + 1))
+        j_quant = ctx.enter_context(tc.tile_pool(name="j_quant", bufs=2 * RUN + 2))
         y_stage = ctx.enter_context(tc.tile_pool(name="y_stage", bufs=3))
         turn_psum = ctx.enter_context(tc.psum_pool(name="turn_psum", bufs=4))
         acc_psum = ctx.enter_context(tc.psum_pool(name="acc_psum", bufs=4))
         ctx.enter_context(tc.manual_schedule())
 
         ident = keep.tile([P, P], F32, name="ident")
-        w_rows = keep.tile([P, K_PASS], BF16, name="w_rows")
+        w_rows = keep.tile([P, SPAN], BF16, name="w_rows")
         w_cols = keep.tile([P, GROUPS, PACK], F32, name="w_cols")
-        j_raw = [keep.tile([P, 2, K], BF16, name="j_raw%d" % i) for i in range(PAIRS)]
+        j_raw = [keep.tile([P, PACK, K], BF16, name="j_raw%d" % g) for g in range(GROUPS)]
         v_raw = [keep.tile([P, PACK, S], BF16, name="v_raw%d" % c) for c in range(PASSES)]
         v_grouped = [keep.tile([P, S, PACK], BF16, name="v_grouped%d" % c, align_bytes=64) for c in range(PASSES)]
         v_codes = [keep.tile([P, S], U32, name="v_codes%d" % c, align_bytes=64) for c in range(PASSES)]
@@ -49,57 +59,57 @@ def tile_weighted_linearised_residual_g2_kernel(tc, jacobian, step, residual, we
         y_codes = [keep.tile([P, S], U32, name="y_codes%d" % g, align_bytes=64) for g in range(GROUPS)]
         y_scales = keep.tile([P, GROUPS, S], U8, name="y_scales", align_bytes=64)
 
-        def group_rows(dram, g):
-            return dram[g * K_PASS:(g + 1) * K_PASS, :].rearrange("(p t) c -> p t c", t=PACK)
+        j_grouped, j_codes, j_scales, acc, y_grouped = {}, {}, {}, {}, {}
 
-        def load_j(pair, lo, hi):
-            g, t0 = divmod(2 * pair, PACK)
-            nc.sync.dma_start(out=j_raw[pair][:, lo:hi, :], in_=group_rows(jacobian, g)[:, t0 + lo:t0 + hi, :])
+        def rows_of(dram, n):
+            return dram[n * SPAN:(n + 1) * SPAN, :].rearrange("(p t) c -> p t c", t=PACK)
+
+        def load_j(g, t_lo, t_hi):
+            nc.sync.dma_start(out=j_raw[g][:, t_lo:t_hi, :], in_=rows_of(jacobian, g)[:, t_lo:t_hi, :])
 
         def load_v(c):
-            nc.sync.dma_start(out=v_raw[c][:], in_=group_rows(step, c))
+            nc.sync.dma_start(out=v_raw[c][:], in_=rows_of(step, c))
 
-        def load_r(g, lo, hi):
-            nc.sync.dma_start(out=r_raw[g][:, lo:hi, :], in_=group_rows(residual, g)[:, lo:hi, :])
+        def load_r(g):
+            nc.sync.dma_start(out=r_raw[g][:], in_=rows_of(residual, g))
 
-        turned = {}
-        grouped = {}
-        j_codes = {}
-        j_scales = {}
-        acc = {}
-        y_grouped = {}
+        def turn_pass(bank, h, rows, c):
+            words = rows.bitcast(F32)
+            for u in range(2):
+                nc.tensor.transpose(bank[:, h, u, :], words[:, PASS_WORDS * c + u:PASS_WORDS * (c + 1):2], ident[:])
 
         def turn(unit):
             bank = turn_psum.tile([P, 2, 2, P], F32, name="bank")
-            turned[unit] = bank
             for h in range(2):
                 tile, c = divmod(2 * unit + h, PASSES)
-                words = j_raw[tile // 2][:, tile % 2, :].bitcast(F32)
-                for u in range(2):
-                    nc.tensor.transpose(bank[:, h, u, :], words[:, 256 * c + u:256 * (c + 1):2], ident[:])
-
-        def empty(unit):
-            dst = j_stage.tile([P, 2 * K_PASS], BF16, name="j_grouped", align_bytes=64)
-            grouped[unit] = dst
+                turn_pass(bank, h, j_raw[tile // PACK][:, tile % PACK, :], c)
+            j_grouped[unit] = j_stage.tile([P, 2 * SPAN], BF16, name="j_grouped", align_bytes=64)
             nc.scalar.copy(
-                out=dst[:].bitcast(F32).rearrange("p (h d u) -> p h d u", h=2, u=2),
-                in_=turned[unit][:].rearrange("p h u d -> p h d u"),
+                out=j_grouped[unit][:].bitcast(F32).rearrange("p (h d u) -> p h d u", h=2, u=2),
+                in_=bank[:].rearrange("p h u d -> p h d u"),
+            )
+
+        def turn_weights():
+            bank = turn_psum.tile([P, 2, 2, P], F32, name="bank")
+            turn_pass(bank, 0, w_rows[:], 0)
+            halfwords = bank[:].rearrange("p h u r -> p (h u r)").bitcast(BF16)
+            nc.scalar.activation(
+                out=w_cols[:].rearrange("p g (u e) -> p u g e", u=2),
+                in_=halfwords.rearrange("p (h u r e) -> p h u r e", h=2, u=2, e=2)[:, 0, :, 0:GROUPS, :],
+                func=COPY,
             )
 
         def quantise_j(unit):
-            codes = j_quant.tile([P, 2 * P], U32, name="j_codes", align_bytes=64)
-            scales = j_quant.tile([P, 2 * P], U8, name="j_scales", align_bytes=64)
-            j_codes[unit] = codes
-            j_scales[unit] = scales
-            nc.vector.quantize_mx(out=codes[:].bitcast(FP8X4), scales=scales[:], in_=grouped[unit][:])
+            j_codes[unit] = j_quant.tile([P, 2 * P], U32, name="j_codes", align_bytes=64)
+            j_scales[unit] = j_quant.tile([P, 2 * P], U8, name="j_scales", align_bytes=64)
+            nc.vector.quantize_mx(out=j_codes[unit][:].bitcast(FP8X4), scales=j_scales[unit][:], in_=j_grouped[unit][:])
 
-        def interleave_v(c, lo, hi, copy):
-            copy(
-                out=v_grouped[c][:, lo:hi, :].rearrange("p (n i) t -> p n t i", i=4),
-                in_=v_raw[c][:, :, lo:hi].rearrange("p t (n i) -> p n t i", i=4),
-            )
+        def interleave(copy, out, in_):
+            copy(out=out.rearrange("p (n i) t -> p n t i", i=4), in_=in_.rearrange("p t (n i) -> p n t i", i=4))
 
-        def quantise_v(c):
+        def prepare_v(c):
+            interleave(nc.scalar.copy, v_grouped[c][:, 0:V_SPLIT, :], v_raw[c][:, :, 0:V_SPLIT])
+            interleave(nc.vector.tensor_copy, v_grouped[c][:, V_SPLIT:S, :], v_raw[c][:, :, V_SPLIT:S])
             nc.vector.quantize_mx(
                 out=v_codes[c][:].bitcast(FP8X4),
                 scales=v_scales[c][:],
@@ -107,7 +117,7 @@ def tile_weighted_linearised_residual_g2_kernel(tc, jacobian, step, residual, we
             )
 
         def multiply(tile, c, lo=0, hi=S):
-            if (tile, lo) not in acc:
+            if c == 0:
                 acc[tile, lo] = acc_psum.tile([P, hi - lo], F32, name="acc")
             unit, h = divmod(PASSES * tile + c, 2)
             cols = slice(h * P, (h + 1) * P)
@@ -125,6 +135,12 @@ def tile_weighted_linearised_residual_g2_kernel(tc, jacobian, step, residual, we
             g, t = divmod(tile, PACK)
             nc.scalar.activation(out=y[g][:, t, :], in_=r_raw[g][:, t, :], func=COPY, scale=w_cols[:, g, t:t + 1])
 
+        def weigh_residual_on_vector(tile):
+            g, t = divmod(tile, PACK)
+            nc.vector.tensor_scalar(
+                out=y[g][:, t, :], in0=r_raw[g][:, t, :], scalar1=w_cols[:, g, t:t + 1], scalar2=None, op0=MULT
+            )
+
         def finish(tile, lo=0, hi=S):
             g, t = divmod(tile, PACK)
             nc.vector.scalar_tensor_tensor(
@@ -132,51 +148,39 @@ def tile_weighted_linearised_residual_g2_kernel(tc, jacobian, step, residual, we
                 op0=MULT, op1=ADD,
             )
 
-        def interleave_y(half, copy):
-            g, h = divmod(half, 2)
-            dst = y_stage.tile([P, HALF, PACK], BF16, name="y_grouped", align_bytes=64)
-            y_grouped[half] = dst
-            copy(
-                out=dst[:].rearrange("p (n i) t -> p n t i", i=4),
-                in_=y[g][:, :, h * HALF:(h + 1) * HALF].rearrange("p t (n i) -> p n t i", i=4),
-            )
+        def interleave_y(g, h, copy):
+            y_grouped[g, h] = y_stage.tile([P, HALF, PACK], BF16, name="y_grouped", align_bytes=64)
+            interleave(copy, y_grouped[g, h][:], y[g][:, :, h * HALF:(h + 1) * HALF])
 
-        def quantise_y(half):
-            g, h = divmod(half, 2)
+        def quantise_y(g, h):
             cols = slice(h * HALF, (h + 1) * HALF)
             nc.vector.quantize_mx(
                 out=y_codes[g][:, cols].bitcast(FP8X4),
                 scales=y_scales[:, g, cols],
-                in_=y_grouped[half][:].rearrange("p n t -> p (n t)"),
+                in_=y_grouped[g, h][:].rearrange("p n t -> p (n t)"),
             )
 
-        def store_y(g, lo, hi, c0=0, c1=S):
-            nc.sync.dma_start(out=group_rows(out_0, g)[:, lo:hi, c0:c1], in_=y[g][:, lo:hi, c0:c1])
+        def store_y(g, t_lo, t_hi, lo=0, hi=S):
+            nc.sync.dma_start(out=rows_of(out_0, g)[:, t_lo:t_hi, lo:hi], in_=y[g][:, t_lo:t_hi, lo:hi])
 
         def store_codes(g, lo=0, hi=S):
-            nc.sync.dma_start(
-                out=out_1[g].rearrange("p m t -> p (m t)").bitcast(I32)[:, lo:hi], in_=y_codes[g][:, lo:hi].bitcast(I32)
-            )
+            words = out_1[g].rearrange("p m t -> p (m t)").bitcast(I32)
+            nc.sync.dma_start(out=words[:, lo:hi], in_=y_codes[g][:, lo:hi].bitcast(I32))
 
-        def store_scales(queue, g_lo, g_hi, quadrants=(0, 1, 2, 3)):
-            scale_rows = out_2.bitcast(I32)
+        def store_scales(queue, g_lo, g_hi, quadrants):
             for q in quadrants:
                 queue.dma_start(
-                    out=scale_rows[g_lo:g_hi, 4 * q:4 * q + 4, :].rearrange("g r m -> r g m"),
+                    out=out_2.bitcast(I32)[g_lo:g_hi, 4 * q:4 * q + 4, :].rearrange("g r m -> r g m"),
                     in_=y_scales[32 * q:32 * q + 4, g_lo:g_hi, :].bitcast(I32),
                 )
 
-        def turn_weights():
-            w_bank = turn_psum.tile([P, 2, 2, P], F32, name="bank")
-            w_words = w_rows[:].bitcast(F32)
-            for u in range(2):
-                nc.tensor.transpose(w_bank[:, 0, u, :], w_words[:, u:256:2], ident[:])
-            nc.scalar.activation(
-                out=w_cols[:].rearrange("p g (u e) -> p u g e", u=2),
-                in_=w_bank[:].rearrange("p h u r -> p (h u r)").bitcast(BF16)
-                .rearrange("p (h u r e) -> p h u r e", h=2, u=2, e=2)[:, 0, :, 0:GROUPS, :],
-                func=COPY,
-            )
+        def finish_and_store(tile):
+            finish(tile)
+            g, t = divmod(tile, PACK)
+            if g == LAST:
+                store_y(g, t, t + 1)
+            elif t == PACK - 1:
+                store_y(g, 0, PACK)
 
         nc.vector.memset(w_rows[:].bitcast(I32), 0)
         make_identity(nc, ident[:])
@@ -186,116 +190,111 @@ def tile_weighted_linearised_residual_g2_kernel(tc, jacobian, step, residual, we
         nc.sync.dma_start(out=w_rows[0:4, :], in_=w_by_group[0:4, :])
         nc.sync.dma_start(out=w_rows[4:GROUPS, :], in_=w_by_group[4:GROUPS, :])
         load_j(0, 1, 2)
-        load_j(1, 0, 1)
+        load_j(0, 2, 3)
         load_v(1)
-        load_j(1, 1, 2)
+        load_j(0, 3, 4)
         load_v(2)
-        load_j(2, 0, 2)
-        load_r(0, 0, 4)
-        load_j(3, 0, 2)
-        for g in range(1, GROUPS):
-            for pair in (2 * g + 2, 2 * g + 3):
-                if pair < PAIRS:
-                    load_j(pair, 0, 2)
-                if pair % 2 == 0:
-                    load_r(g, 0, 4)
+        for g in (1, 2, 3):
+            load_j(g, 0, 2)
+            load_r(g - 1)
+            load_j(g, 2, 4)
+        for g in range(4, GROUPS):
+            load_r(g - 1)
+            load_j(g, 0, PACK)
+        load_r(LAST)
 
-        SPLIT = 192
         turn(0)
-        empty(0)
         quantise_j(0)
-        interleave_v(0, 0, SPLIT, nc.scalar.copy)
-        interleave_v(0, SPLIT, S, nc.vector.tensor_copy)
-        quantise_v(0)
+        prepare_v(0)
         turn_weights()
         for unit in (1, 2, 3):
             turn(unit)
-            empty(unit)
             quantise_j(unit)
-        multiply(0, 0)
-        multiply(1, 0)
-        multiply(2, 0)
-        interleave_v(1, 0, SPLIT, nc.scalar.copy)
-        interleave_v(1, SPLIT, S, nc.vector.tensor_copy)
-        quantise_v(1)
+        for tile in range(HEAD_TILES - 1):
+            multiply(tile, 0)
+        prepare_v(1)
         for unit in (4, 5):
             turn(unit)
-            empty(unit)
             quantise_j(unit)
-        multiply(0, 1)
-        multiply(1, 1)
-        multiply(2, 1)
-        multiply(3, 0)
-        multiply(3, 1)
-        interleave_v(2, 0, SPLIT, nc.scalar.copy)
-        interleave_v(2, SPLIT, S, nc.vector.tensor_copy)
-        quantise_v(2)
-        for unit in (6, 7, 8):
+        for tile in range(HEAD_TILES - 1):
+            multiply(tile, 1)
+        multiply(HEAD_TILES - 1, 0)
+        multiply(HEAD_TILES - 1, 1)
+        prepare_v(2)
+        for unit in range(6, HEAD_UNITS):
             turn(unit)
-            empty(unit)
             quantise_j(unit)
-        for tile in range(4):
-            multiply(tile, 2)
-        for tile in range(3):
+            if unit - 6 < HEAD_WEIGH_ON_VECTOR:
+                weigh_residual_on_vector(unit - 6)
+        for tile in range(HEAD_WEIGH_ON_VECTOR, HEAD_TILES):
             weigh_residual(tile)
+        for tile in range(HEAD_TILES):
+            multiply(tile, 2)
+        for tile in range(HEAD_TILES - 1):
             finish(tile)
-        store_y(0, 0, 2)
-        weigh_residual(3)
 
-        weighed = 4
-        last = GROUPS - 1
-        for i in range(2, PAIRS - 1):
-            a, b = 2 * i, 2 * i + 1
-            units = [3 * (i + 1) + n for n in range(3)]
-            if 2 < i and weighed < 2 * PAIRS:
-                weigh_residual(weighed)
-                weighed += 1
+        held = HEAD_TILES - 1
+        done_group = 0
+        next_slot = PASSES * HEAD_TILES
+        to_weigh = list(range(HEAD_TILES, TILES))
+        starts = list(range(HEAD_UNITS, UNITS, RUN))
+        for first_unit in starts:
+            units = list(range(first_unit, min(first_unit + RUN, UNITS)))
+            is_last = first_unit == starts[-1]
+            before_last = first_unit == starts[-2]
+            end_slot = PASSES * PACK * LAST if before_last else 2 * first_unit
+            weigh_now = to_weigh[:WEIGH_PER_RUN + (1 if first_unit in starts[-3:] else 0)]
+            to_weigh = to_weigh[len(weigh_now):]
+            early = weigh_now[:1] if first_unit > HEAD_UNITS else []
+            for tile in early:
+                weigh_residual(tile)
             for unit in units:
                 turn(unit)
-                empty(unit)
-            for n in range(2 if i % 2 == 0 else 1):
-                if weighed < 2 * PAIRS:
-                    weigh_residual(weighed)
-                    weighed += 1
-            finish(a - 1)
-            store_y((i - 1) // 2, 2 * ((i - 1) % 2), 2 * ((i - 1) % 2) + 2)
-            interleave_y(i - 2, nc.vector.tensor_copy)
-            if i == PAIRS - 2:
-                interleave_y(i - 1, nc.scalar.copy)
-            quantise_j(units[0])
-            quantise_y(i - 2)
-            if i % 2 == 1:
-                store_codes((i - 2) // 2)
-            if i == PAIRS - 3:
-                store_scales(nc.sync, 0, last - 1)
-            for unit in units[1:]:
+            finish_and_store(held)
+            shared = before_last or is_last
+            if shared:
+                interleave_y(done_group, 1, nc.scalar.copy)
+            for tile in weigh_now[len(early):]:
+                weigh_residual(tile)
+            halves = [] if done_group is None else [0] if shared else [0, 1]
+            for n, unit in enumerate(units):
+                if n in halves:
+                    interleave_y(done_group, n, nc.vector.tensor_copy)
                 quantise_j(unit)
-            for tile in (a, b):
-                for c in range(PASSES):
-                    multiply(tile, c)
-            finish(a)
+                if n in halves:
+                    quantise_y(done_group, n)
+                if n == 1 and n in halves:
+                    store_codes(done_group)
 
-        a, b = 2 * PAIRS - 2, 2 * PAIRS - 1
-        store_y(last, 0, 1)
-        finish(a - 1)
-        store_y(last, 1, 2)
-        for lo in (0, HALF):
-            for tile in (a, b):
+            slots = range(next_slot, end_slot)
+            for slot in slots:
+                multiply(*divmod(slot, PASSES))
+            complete = [slot // PASSES for slot in slots if slot % PASSES == PASSES - 1]
+            for tile in complete[:-1]:
+                finish_and_store(tile)
+            if before_last:
+                quantise_y(done_group, 1)
+                store_codes(done_group)
+                store_scales(nc.sync, 0, LAST - 1, range(4))
+            held = complete[-1]
+            groups = [tile // PACK for tile in complete if tile % PACK == PACK - 1]
+            done_group = groups[0] if groups else None
+            next_slot = end_slot
+
+        finish_and_store(held)
+        quantise_y(LAST - 1, 1)
+        store_codes(LAST - 1)
+        for h, copy in enumerate((nc.scalar.copy, nc.vector.tensor_copy)):
+            lo, hi = h * HALF, (h + 1) * HALF
+            for tile in (TILES - 2, TILES - 1):
                 for c in range(PASSES):
-                    multiply(tile, c, lo, lo + HALF)
-        finish(a, 0, HALF)
-        finish(b, 0, HALF)
-        interleave_y(PAIRS - 2, nc.scalar.copy)
-        store_y(last, 2, 4, 0, HALF)
-        quantise_y(PAIRS - 3)
-        store_codes(last - 1)
-        finish(a, HALF, S)
-        finish(b, HALF, S)
-        store_y(last, 2, 4, HALF, S)
-        interleave_y(PAIRS - 1, nc.vector.tensor_copy)
-        quantise_y(PAIRS - 2)
-        store_codes(last, 0, HALF)
-        quantise_y(PAIRS - 1)
-        store_codes(last, HALF, S)
-        store_scales(nc.scalar, last - 1, GROUPS, (0, 1))
-        store_scales(nc.sync, last - 1, GROUPS, (2, 3))
+                    multiply(tile, c, lo, hi)
+                finish(tile, lo, hi)
+            if h == 1:
+                store_y(LAST, 2, PACK)
+            interleave_y(LAST, h, copy)
+        for h in range(2):
+            quantise_y(LAST, h)
+            store_codes(LAST, h * HALF, (h + 1) * HALF)
+        store_scales(nc.scalar, LAST - 1, GROUPS, (0, 1))
+        store_scales(nc.sync, LAST - 1, GROUPS, (2, 3))

@@ -26,6 +26,7 @@ TILES = GROUPS * PACK
 UNITS = TILES * PASSES // 2
 HALF = S // 2
 LAST = GROUPS - 1
+EARLY_GROUPS = GROUPS - 2
 
 RUN = 4
 HEAD_TILES = 4
@@ -57,7 +58,10 @@ def tile_weighted_linearised_residual_g2_kernel(tc, jacobian, step, residual, we
         r_raw = [keep.tile([P, PACK, S], BF16, name="r_raw%d" % g) for g in range(GROUPS)]
         y = [keep.tile([P, PACK, S], F32, name="y%d" % g) for g in range(GROUPS)]
         y_codes = [keep.tile([P, S], U32, name="y_codes%d" % g, align_bytes=64) for g in range(GROUPS)]
-        y_scales = keep.tile([P, GROUPS, S], U8, name="y_scales", align_bytes=64)
+        early_scales = keep.tile([P, EARLY_GROUPS, S], U8, name="early_scales", align_bytes=64)
+        late_scales = keep.tile([P, GROUPS - EARLY_GROUPS, S], U8, name="late_scales", align_bytes=64)
+        y_scales = [early_scales[:, g, :] for g in range(EARLY_GROUPS)]
+        y_scales += [late_scales[:, g, :] for g in range(GROUPS - EARLY_GROUPS)]
 
         j_grouped, j_codes, j_scales, acc, y_grouped = {}, {}, {}, {}, {}
 
@@ -156,7 +160,7 @@ def tile_weighted_linearised_residual_g2_kernel(tc, jacobian, step, residual, we
             cols = slice(h * HALF, (h + 1) * HALF)
             nc.vector.quantize_mx(
                 out=y_codes[g][:, cols].bitcast(FP8X4),
-                scales=y_scales[:, g, cols],
+                scales=y_scales[g][:, cols],
                 in_=y_grouped[g, h][:].rearrange("p n t -> p (n t)"),
             )
 
@@ -167,11 +171,11 @@ def tile_weighted_linearised_residual_g2_kernel(tc, jacobian, step, residual, we
             words = out_1[g].rearrange("p m t -> p (m t)").bitcast(I32)
             nc.sync.dma_start(out=words[:, lo:hi], in_=y_codes[g][:, lo:hi].bitcast(I32))
 
-        def store_scales(queue, g_lo, g_hi, quadrants):
-            for q in quadrants:
+        def store_scales(queue, plane, g_lo, g_hi, rows):
+            for r in rows:
                 queue.dma_start(
-                    out=out_2.bitcast(I32)[g_lo:g_hi, 4 * q:4 * q + 4, :].rearrange("g r m -> r g m"),
-                    in_=y_scales[32 * q:32 * q + 4, g_lo:g_hi, :].bitcast(I32),
+                    out=out_2.bitcast(I32)[g_lo:g_hi, r:16:4, :].rearrange("g q m -> q g m"),
+                    in_=plane[r:P:32, :, :].bitcast(I32),
                 )
 
         def finish_and_store(tile):
@@ -275,7 +279,7 @@ def tile_weighted_linearised_residual_g2_kernel(tc, jacobian, step, residual, we
             if before_last:
                 quantise_y(done_group, 1)
                 store_codes(done_group)
-                store_scales(nc.sync, 0, LAST - 1, range(4))
+                store_scales(nc.sync, early_scales, 0, EARLY_GROUPS, range(4))
             held = complete[-1]
             groups = [tile // PACK for tile in complete if tile % PACK == PACK - 1]
             done_group = groups[0] if groups else None
@@ -296,5 +300,5 @@ def tile_weighted_linearised_residual_g2_kernel(tc, jacobian, step, residual, we
         for h in range(2):
             quantise_y(LAST, h)
             store_codes(LAST, h * HALF, (h + 1) * HALF)
-        store_scales(nc.scalar, LAST - 1, GROUPS, (0, 1))
-        store_scales(nc.sync, LAST - 1, GROUPS, (2, 3))
+        store_scales(nc.scalar, late_scales, EARLY_GROUPS, GROUPS, (0, 1))
+        store_scales(nc.sync, late_scales, EARLY_GROUPS, GROUPS, (2, 3))

from contextlib import ExitStack

import concourse.mybir as mybir
from concourse.masks import make_identity

D, K, S = 3072, 1536, 512
FLOPS = 2 * D * K * S

F32 = mybir.dt.float32
BF16 = mybir.dt.bfloat16
I32 = mybir.dt.int32
U32 = mybir.dt.uint32
U8 = mybir.dt.uint8
FP8X4 = mybir.dt.float8_e4m3fn_x4
COPY = mybir.ActivationFunctionType.Copy
MULT = mybir.AluOpType.mult
ADD = mybir.AluOpType.add

P = 128
PACK = 4
SPAN = P * PACK
PASS_WORDS = SPAN // 2
PASSES = K // SPAN
GROUPS = D // SPAN
TILES = GROUPS * PACK
UNITS = TILES * PASSES // 2
HALF = S // 2
LAST = GROUPS - 1
EARLY_GROUPS = GROUPS - 2

RUN = 4
HEAD_TILES = 4
HEAD_UNITS = 9
WEIGH_PER_RUN = 3
HEAD_WEIGH_ON_VECTOR = 2
V_SPLIT = 224


def tile_weighted_linearised_residual_g2_kernel(tc, jacobian, step, residual, weight, out_0, out_1, out_2):
    nc = tc.nc
    with ExitStack() as ctx:
        keep = ctx.enter_context(tc.tile_pool(name="keep", bufs=1))
        j_stage = ctx.enter_context(tc.tile_pool(name="j_stage", bufs=RUN + 1))
        j_quant = ctx.enter_context(tc.tile_pool(name="j_quant", bufs=2 * RUN + 2))
        y_stage = ctx.enter_context(tc.tile_pool(name="y_stage", bufs=3))
        turn_psum = ctx.enter_context(tc.psum_pool(name="turn_psum", bufs=4))
        acc_psum = ctx.enter_context(tc.psum_pool(name="acc_psum", bufs=4))
        ctx.enter_context(tc.manual_schedule())

        ident = keep.tile([P, P], F32, name="ident")
        w_rows = keep.tile([P, SPAN], BF16, name="w_rows")
        w_cols = keep.tile([P, GROUPS, PACK], F32, name="w_cols")
        j_raw = [keep.tile([P, PACK, K], BF16, name="j_raw%d" % g) for g in range(GROUPS)]
        v_raw = [keep.tile([P, PACK, S], BF16, name="v_raw%d" % c) for c in range(PASSES)]
        v_grouped = [keep.tile([P, S, PACK], BF16, name="v_grouped%d" % c, align_bytes=64) for c in range(PASSES)]
        v_codes = [keep.tile([P, S], U32, name="v_codes%d" % c, align_bytes=64) for c in range(PASSES)]
        v_scales = [keep.tile([P, S], U8, name="v_scales%d" % c, align_bytes=64) for c in range(PASSES)]
        r_raw = [keep.tile([P, PACK, S], BF16, name="r_raw%d" % g) for g in range(GROUPS)]
        y = [keep.tile([P, PACK, S], F32, name="y%d" % g) for g in range(GROUPS)]
        y_codes = [keep.tile([P, S], U32, name="y_codes%d" % g, align_bytes=64) for g in range(GROUPS)]
        early_scales = keep.tile([P, EARLY_GROUPS, S], U8, name="early_scales", align_bytes=64)
        late_scales = keep.tile([P, GROUPS - EARLY_GROUPS, S], U8, name="late_scales", align_bytes=64)
        y_scales = [early_scales[:, g, :] for g in range(EARLY_GROUPS)]
        y_scales += [late_scales[:, g, :] for g in range(GROUPS - EARLY_GROUPS)]

        j_grouped, j_codes, j_scales, acc, y_grouped = {}, {}, {}, {}, {}

        def rows_of(dram, n):
            return dram[n * SPAN:(n + 1) * SPAN, :].rearrange("(p t) c -> p t c", t=PACK)

        def load_j(g, t_lo, t_hi):
            nc.sync.dma_start(out=j_raw[g][:, t_lo:t_hi, :], in_=rows_of(jacobian, g)[:, t_lo:t_hi, :])

        def load_v(c):
            nc.sync.dma_start(out=v_raw[c][:], in_=rows_of(step, c))

        def load_r(g):
            nc.sync.dma_start(out=r_raw[g][:], in_=rows_of(residual, g))

        def turn_pass(bank, h, rows, c):
            words = rows.bitcast(F32)
            for u in range(2):
                nc.tensor.transpose(bank[:, h, u, :], words[:, PASS_WORDS * c + u:PASS_WORDS * (c + 1):2], ident[:])

        def turn(unit):
            bank = turn_psum.tile([P, 2, 2, P], F32, name="bank")
            for h in range(2):
                tile, c = divmod(2 * unit + h, PASSES)
                turn_pass(bank, h, j_raw[tile // PACK][:, tile % PACK, :], c)
            j_grouped[unit] = j_stage.tile([P, 2 * SPAN], BF16, name="j_grouped", align_bytes=64)
            nc.scalar.copy(
                out=j_grouped[unit][:].bitcast(F32).rearrange("p (h d u) -> p h d u", h=2, u=2),
                in_=bank[:].rearrange("p h u d -> p h d u"),
            )

        def turn_weights():
            bank = turn_psum.tile([P, 2, 2, P], F32, name="bank")
            turn_pass(bank, 0, w_rows[:], 0)
            halfwords = bank[:].rearrange("p h u r -> p (h u r)").bitcast(BF16)
            nc.scalar.activation(
                out=w_cols[:].rearrange("p g (u e) -> p u g e", u=2),
                in_=halfwords.rearrange("p (h u r e) -> p h u r e", h=2, u=2, e=2)[:, 0, :, 0:GROUPS, :],
                func=COPY,
            )

        def quantise_j(unit):
            j_codes[unit] = j_quant.tile([P, 2 * P], U32, name="j_codes", align_bytes=64)
            j_scales[unit] = j_quant.tile([P, 2 * P], U8, name="j_scales", align_bytes=64)
            nc.vector.quantize_mx(out=j_codes[unit][:].bitcast(FP8X4), scales=j_scales[unit][:], in_=j_grouped[unit][:])

        def interleave(copy, out, in_):
            copy(out=out.rearrange("p (n i) t -> p n t i", i=4), in_=in_.rearrange("p t (n i) -> p n t i", i=4))

        def prepare_v(c):
            interleave(nc.scalar.copy, v_grouped[c][:, 0:V_SPLIT, :], v_raw[c][:, :, 0:V_SPLIT])
            interleave(nc.vector.tensor_copy, v_grouped[c][:, V_SPLIT:S, :], v_raw[c][:, :, V_SPLIT:S])
            nc.vector.quantize_mx(
                out=v_codes[c][:].bitcast(FP8X4),
                scales=v_scales[c][:],
                in_=v_grouped[c][:].rearrange("p n t -> p (n t)"),
            )

        def multiply(tile, c, lo=0, hi=S):
            if c == 0:
                acc[tile, lo] = acc_psum.tile([P, hi - lo], F32, name="acc")
            unit, h = divmod(PASSES * tile + c, 2)
            cols = slice(h * P, (h + 1) * P)
            nc.tensor.matmul_mx(
                out=acc[tile, lo][:],
                lhsT=j_codes[unit][:, cols].bitcast(FP8X4),
                lhsT_scale=j_scales[unit][:, cols],
                rhs=v_codes[c][:, lo:hi].bitcast(FP8X4),
                rhs_scale=v_scales[c][:, lo:hi],
                start=(c == 0),
                stop=(c == PASSES - 1),
            )

        def weigh_residual(tile):
            g, t = divmod(tile, PACK)
            nc.scalar.activation(out=y[g][:, t, :], in_=r_raw[g][:, t, :], func=COPY, scale=w_cols[:, g, t:t + 1])

        def weigh_residual_on_vector(tile):
            g, t = divmod(tile, PACK)
            nc.vector.tensor_scalar(
                out=y[g][:, t, :], in0=r_raw[g][:, t, :], scalar1=w_cols[:, g, t:t + 1], scalar2=None, op0=MULT
            )

        def finish(tile, lo=0, hi=S):
            g, t = divmod(tile, PACK)
            nc.vector.scalar_tensor_tensor(
                out=y[g][:, t, lo:hi], in0=acc[tile, lo][:], scalar=w_cols[:, g, t:t + 1], in1=y[g][:, t, lo:hi],
                op0=MULT, op1=ADD,
            )

        def interleave_y(g, h, copy):
            y_grouped[g, h] = y_stage.tile([P, HALF, PACK], BF16, name="y_grouped", align_bytes=64)
            interleave(copy, y_grouped[g, h][:], y[g][:, :, h * HALF:(h + 1) * HALF])

        def quantise_y(g, h):
            cols = slice(h * HALF, (h + 1) * HALF)
            nc.vector.quantize_mx(
                out=y_codes[g][:, cols].bitcast(FP8X4),
                scales=y_scales[g][:, cols],
                in_=y_grouped[g, h][:].rearrange("p n t -> p (n t)"),
            )

        def store_y(g, t_lo, t_hi, lo=0, hi=S):
            nc.sync.dma_start(out=rows_of(out_0, g)[:, t_lo:t_hi, lo:hi], in_=y[g][:, t_lo:t_hi, lo:hi])

        def store_codes(g, lo=0, hi=S):
            words = out_1[g].rearrange("p m t -> p (m t)").bitcast(I32)
            nc.sync.dma_start(out=words[:, lo:hi], in_=y_codes[g][:, lo:hi].bitcast(I32))

        def store_scales(queue, plane, g_lo, g_hi, rows):
            for r in rows:
                queue.dma_start(
                    out=out_2.bitcast(I32)[g_lo:g_hi, r:16:4, :].rearrange("g q m -> q g m"),
                    in_=plane[r:P:32, :, :].bitcast(I32),
                )

        def finish_and_store(tile):
            finish(tile)
            g, t = divmod(tile, PACK)
            if g == LAST:
                store_y(g, t, t + 1)
            elif t == PACK - 1:
                store_y(g, 0, PACK)

        nc.vector.memset(w_rows[:].bitcast(I32), 0)
        make_identity(nc, ident[:])
        load_j(0, 0, 1)
        load_v(0)
        w_by_group = weight.rearrange("(g d) -> g d", g=GROUPS)
        nc.sync.dma_start(out=w_rows[0:4, :], in_=w_by_group[0:4, :])
        nc.sync.dma_start(out=w_rows[4:GROUPS, :], in_=w_by_group[4:GROUPS, :])
        load_j(0, 1, 2)
        load_j(0, 2, 3)
        load_v(1)
        load_j(0, 3, 4)
        load_v(2)
        for g in (1, 2, 3):
            load_j(g, 0, 2)
            load_r(g - 1)
            load_j(g, 2, 4)
        for g in range(4, GROUPS):
            load_r(g - 1)
            load_j(g, 0, PACK)
        load_r(LAST)

        turn(0)
        quantise_j(0)
        prepare_v(0)
        turn_weights()
        for unit in (1, 2, 3):
            turn(unit)
            quantise_j(unit)
        for tile in range(HEAD_TILES - 1):
            multiply(tile, 0)
        prepare_v(1)
        for unit in (4, 5):
            turn(unit)
            quantise_j(unit)
        for tile in range(HEAD_TILES - 1):
            multiply(tile, 1)
        multiply(HEAD_TILES - 1, 0)
        multiply(HEAD_TILES - 1, 1)
        prepare_v(2)
        for unit in range(6, HEAD_UNITS):
            turn(unit)
            quantise_j(unit)
            if unit - 6 < HEAD_WEIGH_ON_VECTOR:
                weigh_residual_on_vector(unit - 6)
        for tile in range(HEAD_WEIGH_ON_VECTOR, HEAD_TILES):
            weigh_residual(tile)
        for tile in range(HEAD_TILES):
            multiply(tile, 2)
        for tile in range(HEAD_TILES - 1):
            finish(tile)

        held = HEAD_TILES - 1
        done_group = 0
        next_slot = PASSES * HEAD_TILES
        to_weigh = list(range(HEAD_TILES, TILES))
        starts = list(range(HEAD_UNITS, UNITS, RUN))
        for first_unit in starts:
            units = list(range(first_unit, min(first_unit + RUN, UNITS)))
            is_last = first_unit == starts[-1]
            before_last = first_unit == starts[-2]
            end_slot = PASSES * PACK * LAST if before_last else 2 * first_unit
            weigh_now = to_weigh[:WEIGH_PER_RUN + (1 if first_unit in starts[-3:] else 0)]
            to_weigh = to_weigh[len(weigh_now):]
            early = weigh_now[:1] if first_unit > HEAD_UNITS else []
            for tile in early:
                weigh_residual(tile)
            for unit in units:
                turn(unit)
            finish_and_store(held)
            shared = before_last or is_last
            if shared:
                interleave_y(done_group, 1, nc.scalar.copy)
            for tile in weigh_now[len(early):]:
                weigh_residual(tile)
            halves = [] if done_group is None else [0] if shared else [0, 1]
            for n, unit in enumerate(units):
                if n in halves:
                    interleave_y(done_group, n, nc.vector.tensor_copy)
                quantise_j(unit)
                if n in halves:
                    quantise_y(done_group, n)
                if n == 1 and n in halves:
                    store_codes(done_group)

            slots = range(next_slot, end_slot)
            for slot in slots:
                multiply(*divmod(slot, PASSES))
            complete = [slot // PASSES for slot in slots if slot % PASSES == PASSES - 1]
            for tile in complete[:-1]:
                finish_and_store(tile)
            if before_last:
                quantise_y(done_group, 1)
                store_codes(done_group)
                store_scales(nc.sync, early_scales, 0, EARLY_GROUPS, range(4))
            held = complete[-1]
            groups = [tile // PACK for tile in complete if tile % PACK == PACK - 1]
            done_group = groups[0] if groups else None
            next_slot = end_slot

        finish_and_store(held)
        quantise_y(LAST - 1, 1)
        store_codes(LAST - 1)
        for h, copy in enumerate((nc.scalar.copy, nc.vector.tensor_copy)):
            lo, hi = h * HALF, (h + 1) * HALF
            for tile in (TILES - 2, TILES - 1):
                for c in range(PASSES):
                    multiply(tile, c, lo, hi)
                finish(tile, lo, hi)
            if h == 1:
                store_y(LAST, 2, PACK)
            interleave_y(LAST, h, copy)
        for h in range(2):
            quantise_y(LAST, h)
            store_codes(LAST, h * HALF, (h + 1) * HALF)
        store_scales(nc.scalar, late_scales, EARLY_GROUPS, GROUPS, (0, 1))
        store_scales(nc.sync, late_scales, EARLY_GROUPS, GROUPS, (2, 3))
